import numpy as np
import ml_dtypes


def mxq(x, axis, fmt="e4m3"):
    dtype, down = {"e4m3": (ml_dtypes.float8_e4m3fn, 7), "e5m2": (ml_dtypes.float8_e5m2, 14)}[fmt]
    v = np.moveaxis(np.asarray(x, np.float32).astype(ml_dtypes.bfloat16).astype(np.float64), axis, -1)
    blocks = v.reshape(v.shape[:-1] + (-1, 32))
    amax = np.abs(blocks).max(-1, keepdims=True)
    byte = np.maximum(np.where(amax > 0, np.frexp(amax)[1] - 1 + 127, 0) - down, 1)
    scale = np.exp2(byte - 127.0)
    codes = (blocks / scale).astype(np.float32).astype(dtype).astype(np.float64)
    return np.moveaxis((codes * scale).reshape(v.shape), -1, axis)


WIDE = False


def mx_kscale(k):
    if not WIDE:
        return np.ones(k)
    levels = np.array([30, -30])
    if k % 512:
        return np.exp2(np.random.permutation(np.resize(levels, k // 32))).repeat(32)
    a = np.empty((k // 512, 16))
    for p in range(k // 512):
        a[p, :8] = np.random.permutation(np.resize(levels, 8))
        for g in range(8):
            far = levels[np.abs(levels - a[p, g]) >= 10]
            a[p, g + 8] = far[np.random.randint(len(far))]
    return np.exp2(a.ravel()).repeat(32)


BF16 = ml_dtypes.bfloat16


def bf(x):
    return np.asarray(x, np.float32).astype(BF16)


def f64(x):
    return np.asarray(x).astype(np.float64)


E2M1 = np.array([0.0, 0.5, 1.0, 1.5, 2.0, 3.0, 4.0, 6.0, -0.0, -0.5, -1.0, -1.5, -2.0, -3.0, -4.0, -6.0])


def pack_weight(w, fmt):
    k, n = w.shape
    w = f64(bf(w)).reshape(k // 32, 32, n)
    amax = np.abs(w).max(1)
    if fmt == "e4m3":
        byte = np.frexp(amax)[1] - 1 + 127 - 7
    else:
        mant, ex = np.frexp(amax / 6.0)
        byte = np.where(mant > 0.5, ex, ex - 1) + 127
    byte = np.clip(np.where(amax > 0, byte, 1), 1, 254)
    scaled = (w * np.exp2(127.0 - byte)[:, None, :]).reshape(k, n).astype(np.float32)
    by_word = np.ascontiguousarray(scaled.reshape(k // 512, 128, 4, n).transpose(0, 1, 3, 2))
    if fmt == "e4m3":
        words = by_word.astype(ml_dtypes.float8_e4m3fn).view(np.uint8)
    else:
        c = by_word.astype(ml_dtypes.float4_e2m1fn).view(np.uint8) & 0xF
        words = c[..., 0::2] | (c[..., 1::2] << 4)
    return np.ascontiguousarray(words), np.ascontiguousarray(byte.astype(np.uint8).reshape(k // 512, 16, n))


def unpack_weight(words, scales, fmt):
    g, p, n, _ = words.shape
    if fmt == "e4m3":
        vals = np.ascontiguousarray(words).view(ml_dtypes.float8_e4m3fn).astype(np.float64)
    else:
        nib = np.empty((g, p, n, 4), np.uint8)
        nib[..., 0::2] = words & 0xF
        nib[..., 1::2] = words >> 4
        vals = E2M1[nib]
    vals = vals * np.repeat(np.exp2(scales.astype(np.float64) - 127.0), 8, axis=1)[..., None]
    return vals.transpose(0, 1, 3, 2).reshape(g * 512, n)
def pack4(w):
    words, scales = pack_weight(w, "e2m1")
    return words.reshape(words.shape[0], 128, -1), scales


def unpack4(words, scales):
    return unpack_weight(words.reshape(words.shape[0], 128, -1, 2), scales, "e2m1")


M, P = 2048, 1024


def setup_inputs():
    s, u = mx_kscale(P), mx_kscale(M)
    d = bf((1 + 0.1 * np.random.standard_normal(P)) / s)
    w = bf(np.random.uniform(0.25, 0.45, P))
    a = np.random.standard_normal((P, P))
    omega = (a + a.T) / np.sqrt(2 * P)
    np.fill_diagonal(omega, f64(w))
    theta_words, theta_scales = pack4(f64(d)[:, None] * omega)
    return {"x": bf(np.random.standard_normal((M, P)) / f64(d) * u[:, None]),
            "theta_words": theta_words,
            "theta_scales": theta_scales,
            "v": bf(0.3 * np.exp(0.5 * np.random.standard_normal(M)) / np.sqrt(M) / u ** 2),
            "d": d,
            "w": w}


def reference(x, theta_words, theta_scales, v, d, w):
    x = f64(x)
    theta = unpack4(theta_words, theta_scales)
    r = (mxq(x, 1, "e4m3") @ theta) * f64(v)[:, None]
    c = (mxq(x, 0, "e4m3").T @ mxq(r, 0, "e5m2")) * f64(d)[:, None]
    return c + c.T - np.diag(1 / f64(w))

@@ -1,0 +1,295 @@
+from contextlib import ExitStack
+
+import concourse.mybir as mybir
+from concourse.masks import make_identity
+
+M, P = 2048, 1024
+FLOPS = 2 * M * P * P * 2
+
+F32 = mybir.dt.float32
+BF16 = mybir.dt.bfloat16
+I32 = mybir.dt.int32
+U32 = mybir.dt.uint32
+U8 = mybir.dt.uint8
+E4M3 = mybir.dt.float8_e4m3fn_x4
+E5M2 = mybir.dt.float8_e5m2_x4
+E2M1 = mybir.dt.float4_e2m1fn_x4
+COPY = mybir.ActivationFunctionType.Copy
+MULT = mybir.AluOpType.mult
+ADD = mybir.AluOpType.add
+
+LANES = 128
+PACK = 4
+PASS = LANES * PACK
+HALF = P // 2
+GROUPS = M // PASS
+KPASSES = P // PASS
+TILES = HALF // LANES
+BANKS = 8
+LOW, HIGH = 0, 1
+
+
+def tile_concord_graph_gradient_s9_kernel(tc, x, theta_words, theta_scales, v, d, w, out):
+    nc = tc.nc
+    with ExitStack() as ctx:
+        sb = ctx.enter_context(tc.tile_pool(name="sb", bufs=1))
+        ps = ctx.enter_context(tc.psum_pool(name="ps", bufs=1))
+        ctx.enter_context(tc.manual_schedule())
+
+        def tiles(name, count, shape, dtype):
+            return [sb.tile(shape, dtype, name="%s%d" % (name, n), align_bytes=64) for n in range(count)]
+
+        banks = [ps.tile([LANES, HALF], F32, name="bank%d" % n) for n in range(BANKS)]
+        taken = []
+
+        def take_bank():
+            taken.append(banks[len(taken) % BANKS])
+            return taken[-1]
+
+        ident = sb.tile([LANES, LANES], F32, name="ident", align_bytes=64)
+        ident16 = sb.tile([LANES, LANES], BF16, name="ident16", align_bytes=64)
+        xs = tiles("xs", GROUPS, [LANES, PACK * P], BF16)
+        theta = tiles("theta", 2, [LANES, KPASSES, 2 * HALF], U8)
+        theta_plane = sb.tile([LANES, KPASSES, P], U8, name="theta_plane", align_bytes=64)
+        v16 = sb.tile([LANES, GROUPS, PACK], BF16, name="v16", align_bytes=64)
+        v32 = sb.tile([LANES, GROUPS * PACK], F32, name="v32", align_bytes=64)
+        dw_rows = sb.tile([LANES, LANES], BF16, name="dw_rows", align_bytes=64)
+        d_col = sb.tile([LANES, 2 * TILES], F32, name="d_col", align_bytes=64)
+        neg_w = sb.tile([LANES, 2 * TILES], F32, name="neg_w", align_bytes=64)
+        neg_inv_w = sb.tile([LANES, 2 * TILES], F32, name="neg_inv_w", align_bytes=64)
+        d_row = sb.tile([LANES, HALF], BF16, name="d_row", align_bytes=64)
+        x1_in = tiles("x1_in", PACK, [LANES, KPASSES * PASS], BF16)
+        x1_codes = tiles("x1_codes", 2 * PACK, [LANES, KPASSES * LANES], U32)
+        x1_plane = tiles("x1_plane", 2 * PACK, [LANES, KPASSES * LANES], U8)
+        r_rows = tiles("r_rows", 3, [LANES, PACK * HALF], BF16)
+        r_in = tiles("r_in", 2, [LANES, PACK * HALF], BF16)
+        x2_in = tiles("x2_in", 3, [LANES, PACK * HALF], BF16)
+        r_codes = tiles("r_codes", 2 * GROUPS, [LANES, HALF], U32)
+        r_plane = tiles("r_plane", 2 * GROUPS, [LANES, HALF], U8)
+        x2_codes = tiles("x2_codes", 2 * GROUPS, [LANES, HALF], U32)
+        x2_plane = tiles("x2_plane", 2 * GROUPS, [LANES, HALF], U8)
+        scaled = tiles("scaled", 2 * TILES, [LANES, HALF], F32)
+        upper_t = tiles("upper_t", TILES, [LANES, HALF], F32)
+        diag_out = tiles("diag_out", 2 * TILES, [LANES, HALF], F32)
+        lower_out = tiles("lower_out", TILES, [LANES, HALF], F32)
+        upper_out = tiles("upper_out", TILES, [LANES, HALF], F32)
+
+        def load_x(g, t0, t1):
+            rows = x[g * PASS:(g + 1) * PASS, :].rearrange("(p t) k -> p (t k)", t=PACK)
+            nc.sync.dma_start(out=xs[g][:, t0 * P:t1 * P], in_=rows[:, t0 * P:t1 * P])
+
+        def load_theta(half):
+            words = theta_words.rearrange("h p b -> p h b")[:, :, half * 2 * HALF:(half + 1) * 2 * HALF]
+            nc.sync.dma_start(out=theta[half][:].bitcast(I32), in_=words.bitcast(I32))
+
+        make_identity(nc, ident[:])
+        nc.vector.memset(theta_plane[:].rearrange("p h n -> p (h n)").bitcast(I32), 0)
+        load_x(0, 0, 1)
+        load_x(0, 1, 2)
+        for q in range(4):
+            rows = theta_scales[:, 4 * q:4 * q + 4, :].rearrange("h r n -> r h n")
+            nc.scalar.dma_start(out=theta_plane[32 * q:32 * q + 4, :, :].bitcast(I32), in_=rows.bitcast(I32))
+        load_x(0, 2, 4)
+        load_theta(LOW)
+        nc.gpsimd.dma_start(out=v16[:], in_=v.rearrange("(g p t) -> p g t", g=GROUPS, t=PACK))
+        nc.gpsimd.memset(dw_rows[:], 0.0)
+        nc.gpsimd.dma_start(out=dw_rows[0:8, :], in_=d.rearrange("(c j) -> c j", j=LANES))
+        nc.gpsimd.dma_start(out=dw_rows[8:16, :], in_=w.rearrange("(c j) -> c j", j=LANES))
+        load_x(1, 0, 2)
+        load_theta(HIGH)
+        load_x(1, 2, 4)
+        load_x(2, 0, 4)
+        load_x(3, 0, 4)
+        nc.sync.dma_start(out=d_row[:], in_=d[0:HALF].partition_broadcast(LANES))
+        nc.scalar.activation(out=ident16[:], in_=ident[:], func=COPY)
+
+        def turn_x(g, t):
+            bank = take_bank()
+            words = xs[g][:].bitcast(F32)
+            for h in range(KPASSES):
+                for u in range(2):
+                    first = t * (P // 2) + h * 2 * LANES
+                    n = 2 * h + u
+                    nc.tensor.transpose(bank[:, n * LANES:(n + 1) * LANES],
+                                        words[:, first + u:first + 2 * LANES:2], ident[:])
+            nc.scalar.copy(out=x1_in[t][:].bitcast(F32).rearrange("p (h r u) -> p h r u", h=KPASSES, u=2),
+                           in_=bank[:].rearrange("p (h u r) -> p h r u", h=KPASSES, u=2))
+
+        def quantize_x1(g, t):
+            n = (g * PACK + t) % (2 * PACK)
+            nc.vector.quantize_mx(out=x1_codes[n][:].bitcast(E4M3), scales=x1_plane[n][:], in_=x1_in[t][:])
+
+        def residuals(g, half, t):
+            bank = take_bank()
+            n = (g * PACK + t) % (2 * PACK)
+            for h in range(KPASSES):
+                cols = slice(h * LANES, (h + 1) * LANES)
+                nc.tensor.matmul_mx(out=bank[:], lhsT=x1_codes[n][:, cols].bitcast(E4M3), lhsT_scale=x1_plane[n][:, cols],
+                                    rhs=theta[half][:, h, :].bitcast(E2M1),
+                                    rhs_scale=theta_plane[:, h, half * HALF:(half + 1) * HALF],
+                                    start=(h == 0), stop=(h == KPASSES - 1))
+            rows = r_rows[(2 * g + half) % 3]
+            nc.scalar.activation(out=rows[:, t * HALF:(t + 1) * HALF], in_=bank[:], func=COPY,
+                                 scale=v32[:, g * PACK + t:g * PACK + t + 1])
+
+        def interleave(engine_copy, dst, src_rows):
+            engine_copy(out=dst[:].rearrange("p (c i t) -> p c t i", i=4, t=PACK),
+                        in_=src_rows.rearrange("p t (c i) -> p c t i", i=4))
+
+        def interleave_r(g, half):
+            rows = r_rows[(2 * g + half) % 3][:].rearrange("p (t n) -> p t n", t=PACK)
+            interleave(nc.vector.tensor_copy, r_in[half], rows)
+
+        def quantize_r(g, half):
+            n = 2 * g + half
+            nc.vector.quantize_mx(out=r_codes[n][:].bitcast(E5M2), scales=r_plane[n][:], in_=r_in[half][:])
+
+        def interleave_x2(engine_copy, g, half):
+            rows = xs[g][:].rearrange("p (t k) -> p t k", t=PACK)[:, :, half * HALF:(half + 1) * HALF]
+            interleave(engine_copy, x2_in[(half * GROUPS + g) % 3], rows)
+
+        def quantize_x2(g, half):
+            n = 2 * g + half
+            nc.vector.quantize_mx(out=x2_codes[n][:].bitcast(E4M3), scales=x2_plane[n][:],
+                                  in_=x2_in[(half * GROUPS + g) % 3][:])
+
+        def x2_times_r(bank, g, x2_half, tile, r_half):
+            cols = slice(tile * LANES, (tile + 1) * LANES)
+            a, b = 2 * g + x2_half, 2 * g + r_half
+            nc.tensor.matmul_mx(out=bank[:], lhsT=x2_codes[a][:, cols].bitcast(E4M3), lhsT_scale=x2_plane[a][:, cols],
+                                rhs=r_codes[b][:].bitcast(E5M2), rhs_scale=r_plane[b][:],
+                                start=(g == 0), stop=(g == GROUPS - 1))
+
+        def r_times_x2(bank, g, tile):
+            cols = slice(tile * LANES, (tile + 1) * LANES)
+            a, b = 2 * g + HIGH, 2 * g + LOW
+            nc.tensor.matmul_mx(out=bank[:], lhsT=r_codes[a][:, cols].bitcast(E5M2), lhsT_scale=r_plane[a][:, cols],
+                                rhs=x2_codes[b][:].bitcast(E4M3), rhs_scale=x2_plane[b][:],
+                                start=(g == 0), stop=(g == GROUPS - 1))
+
+        def turn_dw():
+            bank = take_bank()
+            cols = bank[:].bitcast(BF16)[:, 0:LANES]
+            nc.tensor.transpose(cols, dw_rows[:], ident16[:])
+            nc.scalar.copy(out=d_col[:], in_=cols[:, 0:8])
+            nc.scalar.activation(out=neg_w[:], in_=cols[:, 8:16], func=COPY, scale=-1.0)
+
+        def scale_diag(half, group_banks, tile):
+            n = half * TILES + tile
+            nc.scalar.activation(out=scaled[n][:], in_=group_banks[tile][:], func=COPY, scale=d_col[:, n:n + 1])
+
+        def turn_diag(half, tile):
+            bank = take_bank()
+            for j in range(TILES):
+                nc.tensor.transpose(bank[:, j * LANES:(j + 1) * LANES],
+                                    scaled[half * TILES + j][:, tile * LANES:(tile + 1) * LANES], ident[:])
+            n = half * TILES + tile
+            nc.vector.tensor_tensor(out=diag_out[n][:], in0=bank[:], in1=scaled[n][:], op=ADD)
+
+        def finish_diag(half, tile):
+            n = half * TILES + tile
+            block = diag_out[n][:, tile * LANES:(tile + 1) * LANES]
+            nc.vector.scalar_tensor_tensor(out=block, in0=ident[:], scalar=neg_inv_w[:, n:n + 1], in1=block,
+                                           op0=MULT, op1=ADD)
+            nc.sync.dma_start(out=out[n * LANES:(n + 1) * LANES, half * HALF:(half + 1) * HALF], in_=diag_out[n][:])
+
+        def lower(tile):
+            bank = take_bank()
+            for g in range(GROUPS):
+                x2_times_r(bank, g, HIGH, tile, LOW)
+            n = TILES + tile
+            nc.vector.scalar_tensor_tensor(out=lower_out[tile][:], in0=bank[:], scalar=d_col[:, n:n + 1],
+                                           in1=upper_t[tile][:], op0=MULT, op1=ADD)
+            nc.sync.dma_start(out=out[n * LANES:(n + 1) * LANES, 0:HALF], in_=lower_out[tile][:])
+
+        def upper(tile):
+            bank = take_bank()
+            for i in range(TILES):
+                nc.tensor.transpose(bank[:, i * LANES:(i + 1) * LANES],
+                                    lower_out[tile][:, i * LANES:(i + 1) * LANES], ident[:])
+            nc.scalar.copy(out=upper_out[tile][:], in_=bank[:])
+            n = TILES + tile
+            nc.sync.dma_start(out=out[0:HALF, n * LANES:(n + 1) * LANES].rearrange("(i p) c -> p i c", p=LANES),
+                              in_=upper_out[tile][:].rearrange("p (i c) -> p i c", i=TILES))
+
+        for t in range(PACK):
+            turn_x(0, t)
+            quantize_x1(0, t)
+            if t == 1:
+                nc.vector.tensor_copy(out=v32[:], in_=v16[:].rearrange("p g t -> p (g t)"))
+        for g in range(GROUPS):
+            more = g + 1 < GROUPS
+            for t in range(PACK):
+                residuals(g, LOW, t)
+            if g > 0:
+                interleave_r(g - 1, HIGH)
+            interleave_x2(nc.vector.tensor_copy, g, LOW)
+            if g > 0:
+                quantize_r(g - 1, HIGH)
+            interleave_r(g, LOW)
+            quantize_x2(g, LOW)
+            if more:
+                for t in range(PACK):
+                    turn_x(g + 1, t)
+            if g == 1:
+                turn_dw()
+            if more:
+                quantize_x1(g + 1, 0)
+            quantize_r(g, LOW)
+            if more:
+                for t in range(1, PACK):
+                    quantize_x1(g + 1, t)
+            if g == 1:
+                nc.vector.reciprocal(out=neg_inv_w[:], in_=neg_w[:])
+            for t in range(PACK):
+                residuals(g, HIGH, t)
+
+        def upper_transposed(tile):
+            bank = take_bank()
+            for g in range(GROUPS):
+                r_times_x2(bank, g, tile)
+            nc.vector.tensor_tensor(out=upper_t[tile][:], in0=bank[:], in1=d_row[:], op=MULT)
+
+        def diag_rows(half):
+            for tile in range(TILES):
+                turn_diag(half, tile)
+                if tile > 0:
+                    finish_diag(half, tile - 1)
+            finish_diag(half, TILES - 1)
+
+        last = GROUPS - 1
+        interleave_r(last, HIGH)
+        interleave_x2(nc.scalar.copy, 0, HIGH)
+        interleave_x2(nc.vector.tensor_copy, 1, HIGH)
+        quantize_r(last, HIGH)
+        low_banks = [take_bank() for tile in range(TILES)]
+        for g in range(GROUPS):
+            for tile in range(TILES):
+                x2_times_r(low_banks[tile], g, LOW, tile, LOW)
+        quantize_x2(0, HIGH)
+        quantize_x2(1, HIGH)
+        for tile in range(TILES):
+            scale_diag(LOW, low_banks, tile)
+        interleave_x2(nc.vector.tensor_copy, 2, HIGH)
+        interleave_x2(nc.scalar.copy, 3, HIGH)
+        upper_transposed(0)
+        quantize_x2(2, HIGH)
+        upper_transposed(1)
+        quantize_x2(3, HIGH)
+        diag_rows(LOW)
+        for tile in range(TILES):
+            bank = take_bank()
+            for g in range(GROUPS):
+                x2_times_r(bank, g, HIGH, tile, HIGH)
+            scale_diag(HIGH, {tile: bank}, tile)
+        lower(0)
+        lower(1)
+        diag_rows(HIGH)
+        upper(0)
+        upper(1)
+        upper_transposed(2)
+        upper_transposed(3)
+        lower(2)
+        lower(3)
+        upper(2)
+        upper(3)

@@ -72,7 +72,7 @@ def tile_concord_graph_gradient_s9_kernel(tc, x, theta_words, theta_scales, v, d
         upper_t = tiles("upper_t", TILES, [LANES, HALF], F32)
         diag_out = tiles("diag_out", 2 * TILES, [LANES, HALF], F32)
         lower_out = tiles("lower_out", TILES, [LANES, HALF], F32)
-        upper_out = tiles("upper_out", TILES, [LANES, HALF], F32)
+        upper_out = sb.tile([LANES, TILES, HALF], F32, name="upper_out", align_bytes=64)
 
         def load_x(g, t0, t1):
             rows = x[g * PASS:(g + 1) * PASS, :].rearrange("(p t) k -> p (t k)", t=PACK)
@@ -146,12 +146,12 @@ def tile_concord_graph_gradient_s9_kernel(tc, x, theta_words, theta_scales, v, d
 
         def interleave_x2(engine_copy, g, half):
             rows = xs[g][:].rearrange("p (t k) -> p t k", t=PACK)[:, :, half * HALF:(half + 1) * HALF]
-            interleave(engine_copy, x2_in[(half * GROUPS + g) % 3], rows)
+            interleave(engine_copy, x2_in[(half + g) % 3], rows)
 
         def quantize_x2(g, half):
             n = 2 * g + half
             nc.vector.quantize_mx(out=x2_codes[n][:].bitcast(E4M3), scales=x2_plane[n][:],
-                                  in_=x2_in[(half * GROUPS + g) % 3][:])
+                                  in_=x2_in[(half + g) % 3][:])
 
         def x2_times_r(bank, g, x2_half, tile, r_half):
             cols = slice(tile * LANES, (tile + 1) * LANES)
@@ -193,30 +193,37 @@ def tile_concord_graph_gradient_s9_kernel(tc, x, theta_words, theta_scales, v, d
                                            op0=MULT, op1=ADD)
             nc.sync.dma_start(out=out[n * LANES:(n + 1) * LANES, half * HALF:(half + 1) * HALF], in_=diag_out[n][:])
 
-        def lower(tile):
+        def lower(tile, parts):
             bank = take_bank()
             for g in range(GROUPS):
                 x2_times_r(bank, g, HIGH, tile, LOW)
             n = TILES + tile
-            nc.vector.scalar_tensor_tensor(out=lower_out[tile][:], in0=bank[:], scalar=d_col[:, n:n + 1],
-                                           in1=upper_t[tile][:], op0=MULT, op1=ADD)
+            width = HALF // parts
+            for part in range(parts):
+                cols = slice(part * width, (part + 1) * width)
+                nc.vector.scalar_tensor_tensor(out=lower_out[tile][:, cols], in0=bank[:, cols], scalar=d_col[:, n:n + 1],
+                                               in1=upper_t[tile][:, cols], op0=MULT, op1=ADD)
             nc.sync.dma_start(out=out[n * LANES:(n + 1) * LANES, 0:HALF], in_=lower_out[tile][:])
 
-        def upper(tile):
+        def upper(tile, first, count):
             bank = take_bank()
-            for i in range(TILES):
+            for i in range(count):
                 nc.tensor.transpose(bank[:, i * LANES:(i + 1) * LANES],
-                                    lower_out[tile][:, i * LANES:(i + 1) * LANES], ident[:])
-            nc.scalar.copy(out=upper_out[tile][:], in_=bank[:])
-            n = TILES + tile
-            nc.sync.dma_start(out=out[0:HALF, n * LANES:(n + 1) * LANES].rearrange("(i p) c -> p i c", p=LANES),
-                              in_=upper_out[tile][:].rearrange("p (i c) -> p i c", i=TILES))
+                                    lower_out[tile][:, (first + i) * LANES:(first + i + 1) * LANES], ident[:])
+            nc.scalar.copy(out=upper_out[:, first:first + count, tile * LANES:(tile + 1) * LANES],
+                           in_=bank[:, 0:count * LANES].rearrange("p (i c) -> p i c", i=count))
+
+        def store_upper(queue, first, count, tile, width):
+            rows = out[first * LANES:(first + count) * LANES, HALF + tile * LANES:HALF + (tile + width) * LANES]
+            queue.dma_start(out=rows.rearrange("(i p) c -> p i c", p=LANES),
+                            in_=upper_out[:, first:first + count, tile * LANES:(tile + width) * LANES])
 
         for t in range(PACK):
             turn_x(0, t)
             quantize_x1(0, t)
             if t == 1:
                 nc.vector.tensor_copy(out=v32[:], in_=v16[:].rearrange("p g t -> p (g t)"))
+        interleave_x2(nc.vector.tensor_copy, 0, HIGH)
         for g in range(GROUPS):
             more = g + 1 < GROUPS
             for t in range(PACK):
@@ -226,23 +233,31 @@ def tile_concord_graph_gradient_s9_kernel(tc, x, theta_words, theta_scales, v, d
             interleave_x2(nc.vector.tensor_copy, g, LOW)
             if g > 0:
                 quantize_r(g - 1, HIGH)
+            else:
+                quantize_x2(0, HIGH)
             interleave_r(g, LOW)
             quantize_x2(g, LOW)
             if more:
-                for t in range(PACK):
-                    turn_x(g + 1, t)
-            if g == 1:
-                turn_dw()
-            if more:
+                turn_x(g + 1, 0)
+                turn_x(g + 1, 1)
                 quantize_x1(g + 1, 0)
             quantize_r(g, LOW)
             if more:
-                for t in range(1, PACK):
-                    quantize_x1(g + 1, t)
-            if g == 1:
+                quantize_x1(g + 1, 1)
+            residuals(g, HIGH, 0)
+            residuals(g, HIGH, 1)
+            if more:
+                turn_x(g + 1, 2)
+                turn_x(g + 1, 3)
+            if g == 2:
+                turn_dw()
+            if more:
+                quantize_x1(g + 1, 2)
+                quantize_x1(g + 1, 3)
+            if g == 2:
                 nc.vector.reciprocal(out=neg_inv_w[:], in_=neg_w[:])
-            for t in range(PACK):
-                residuals(g, HIGH, t)
+            residuals(g, HIGH, 2)
+            residuals(g, HIGH, 3)
 
         def upper_transposed(tile):
             bank = take_bank()
@@ -259,37 +274,40 @@ def tile_concord_graph_gradient_s9_kernel(tc, x, theta_words, theta_scales, v, d
 
         last = GROUPS - 1
         interleave_r(last, HIGH)
-        interleave_x2(nc.scalar.copy, 0, HIGH)
-        interleave_x2(nc.vector.tensor_copy, 1, HIGH)
+        interleave_x2(nc.scalar.copy, 1, HIGH)
+        interleave_x2(nc.vector.tensor_copy, 2, HIGH)
         quantize_r(last, HIGH)
         low_banks = [take_bank() for tile in range(TILES)]
         for g in range(GROUPS):
             for tile in range(TILES):
                 x2_times_r(low_banks[tile], g, LOW, tile, LOW)
-        quantize_x2(0, HIGH)
+        quantize_x2(2, HIGH)
         quantize_x2(1, HIGH)
         for tile in range(TILES):
             scale_diag(LOW, low_banks, tile)
-        interleave_x2(nc.vector.tensor_copy, 2, HIGH)
-        interleave_x2(nc.scalar.copy, 3, HIGH)
+        interleave_x2(nc.vector.tensor_copy, 3, HIGH)
         upper_transposed(0)
-        quantize_x2(2, HIGH)
-        upper_transposed(1)
         quantize_x2(3, HIGH)
+        upper_transposed(1)
         diag_rows(LOW)
         for tile in range(TILES):
             bank = take_bank()
             for g in range(GROUPS):
                 x2_times_r(bank, g, HIGH, tile, HIGH)
             scale_diag(HIGH, {tile: bank}, tile)
-        lower(0)
-        lower(1)
+        lower(0, 1)
         diag_rows(HIGH)
-        upper(0)
-        upper(1)
+        lower(1, 1)
         upper_transposed(2)
+        lower(2, 1)
         upper_transposed(3)
-        lower(2)
-        lower(3)
-        upper(2)
-        upper(3)
+        upper(0, 0, TILES)
+        upper(1, 0, TILES)
+        store_upper(nc.sync, 0, TILES, 0, 2)
+        upper(2, 0, TILES)
+        store_upper(nc.sync, 0, TILES, 2, 1)
+        lower(3, 2)
+        upper(3, 0, 2)
+        store_upper(nc.sync, 0, 2, 3, 1)
+        upper(3, 2, 2)
+        store_upper(nc.scalar, 2, 2, 3, 1)

@@ -27,6 +27,7 @@ KPASSES = P // PASS
 TILES = HALF // LANES
 BANKS = 8
 LOW, HIGH = 0, 1
+WARM_PASSES = 3
 
 
 def tile_concord_graph_gradient_s9_kernel(tc, x, theta_words, theta_scales, v, d, w, out):
@@ -58,6 +59,9 @@ def tile_concord_graph_gradient_s9_kernel(tc, x, theta_words, theta_scales, v, d
         neg_w = sb.tile([LANES, 2 * TILES], F32, name="neg_w", align_bytes=64)
         neg_inv_w = sb.tile([LANES, 2 * TILES], F32, name="neg_inv_w", align_bytes=64)
         d_row = sb.tile([LANES, HALF], BF16, name="d_row", align_bytes=64)
+        warm_in = sb.tile([LANES, PASS], BF16, name="warm_in", align_bytes=64)
+        warm_codes = sb.tile([LANES, HALF + LANES], U32, name="warm_codes", align_bytes=64)
+        warm_plane = sb.tile([LANES, HALF + LANES], U8, name="warm_plane", align_bytes=64)
         x1_in = tiles("x1_in", PACK, [LANES, KPASSES * PASS], BF16)
         x1_codes = tiles("x1_codes", 2 * PACK, [LANES, KPASSES * LANES], U32)
         x1_plane = tiles("x1_plane", 2 * PACK, [LANES, KPASSES * LANES], U8)
@@ -82,28 +86,39 @@ def tile_concord_graph_gradient_s9_kernel(tc, x, theta_words, theta_scales, v, d
             words = theta_words.rearrange("h p b -> p h b")[:, :, half * 2 * HALF:(half + 1) * 2 * HALF]
             nc.sync.dma_start(out=theta[half][:].bitcast(I32), in_=words.bitcast(I32))
 
+        nc.gpsimd.memset(theta_plane[:].rearrange("p h n -> p (h n)").bitcast(I32), 0)
+        nc.gpsimd.memset(warm_in[:], 0.0)
         make_identity(nc, ident[:])
-        nc.vector.memset(theta_plane[:].rearrange("p h n -> p (h n)").bitcast(I32), 0)
+        nc.gpsimd.dma_start(out=v16[:], in_=v.rearrange("(g p t) -> p g t", g=GROUPS, t=PACK))
+        nc.gpsimd.memset(dw_rows[:], 0.0)
         load_x(0, 0, 1)
         load_x(0, 1, 2)
         for q in range(4):
             rows = theta_scales[:, 4 * q:4 * q + 4, :].rearrange("h r n -> r h n")
-            nc.scalar.dma_start(out=theta_plane[32 * q:32 * q + 4, :, :].bitcast(I32), in_=rows.bitcast(I32))
-        load_x(0, 2, 4)
+            nc.sync.dma_start(out=theta_plane[32 * q:32 * q + 4, :, :].bitcast(I32), in_=rows.bitcast(I32))
+        load_x(0, 2, 3)
+        load_x(0, 3, 4)
         load_theta(LOW)
-        nc.gpsimd.dma_start(out=v16[:], in_=v.rearrange("(g p t) -> p g t", g=GROUPS, t=PACK))
-        nc.gpsimd.memset(dw_rows[:], 0.0)
-        nc.gpsimd.dma_start(out=dw_rows[0:8, :], in_=d.rearrange("(c j) -> c j", j=LANES))
-        nc.gpsimd.dma_start(out=dw_rows[8:16, :], in_=w.rearrange("(c j) -> c j", j=LANES))
         load_x(1, 0, 2)
-        load_theta(HIGH)
         load_x(1, 2, 4)
+        load_theta(HIGH)
         load_x(2, 0, 4)
         load_x(3, 0, 4)
+        nc.sync.dma_start(out=dw_rows[0:8, :], in_=d.rearrange("(c j) -> c j", j=LANES))
+        nc.sync.dma_start(out=dw_rows[8:16, :], in_=w.rearrange("(c j) -> c j", j=LANES))
         nc.sync.dma_start(out=d_row[:], in_=d[0:HALF].partition_broadcast(LANES))
         nc.scalar.activation(out=ident16[:], in_=ident[:], func=COPY)
 
-        def turn_x(g, t):
+        nc.vector.quantize_mx(out=warm_codes[:, HALF:].bitcast(E4M3), scales=warm_plane[:, HALF:], in_=warm_in[:])
+        for n in range(TILES):
+            cols = slice(n * LANES, (n + 1) * LANES)
+            nc.vector.quantize_mx(out=warm_codes[:, cols].bitcast(E5M2), scales=warm_plane[:, cols], in_=warm_in[:])
+        for n in range(WARM_PASSES):
+            nc.tensor.matmul_mx(out=banks[-1][:], lhsT=warm_codes[:, HALF:].bitcast(E4M3), lhsT_scale=warm_plane[:, HALF:],
+                                rhs=warm_codes[:, 0:HALF].bitcast(E5M2), rhs_scale=warm_plane[:, 0:HALF],
+                                start=True, stop=True)
+
+        def turn_x(g, t, engine_copy):
             bank = take_bank()
             words = xs[g][:].bitcast(F32)
             for h in range(KPASSES):
@@ -112,7 +127,7 @@ def tile_concord_graph_gradient_s9_kernel(tc, x, theta_words, theta_scales, v, d
                     n = 2 * h + u
                     nc.tensor.transpose(bank[:, n * LANES:(n + 1) * LANES],
                                         words[:, first + u:first + 2 * LANES:2], ident[:])
-            nc.scalar.copy(out=x1_in[t][:].bitcast(F32).rearrange("p (h r u) -> p h r u", h=KPASSES, u=2),
+            engine_copy(out=x1_in[t][:].bitcast(F32).rearrange("p (h r u) -> p h r u", h=KPASSES, u=2),
                            in_=bank[:].rearrange("p (h u r) -> p h r u", h=KPASSES, u=2))
 
         def quantize_x1(g, t):
@@ -205,12 +220,12 @@ def tile_concord_graph_gradient_s9_kernel(tc, x, theta_words, theta_scales, v, d
                                                in1=upper_t[tile][:, cols], op0=MULT, op1=ADD)
             nc.sync.dma_start(out=out[n * LANES:(n + 1) * LANES, 0:HALF], in_=lower_out[tile][:])
 
-        def upper(tile, first, count):
+        def upper(tile, first, count, engine_copy):
             bank = take_bank()
             for i in range(count):
                 nc.tensor.transpose(bank[:, i * LANES:(i + 1) * LANES],
                                     lower_out[tile][:, (first + i) * LANES:(first + i + 1) * LANES], ident[:])
-            nc.scalar.copy(out=upper_out[:, first:first + count, tile * LANES:(tile + 1) * LANES],
+            engine_copy(out=upper_out[:, first:first + count, tile * LANES:(tile + 1) * LANES],
                            in_=bank[:, 0:count * LANES].rearrange("p (i c) -> p i c", i=count))
 
         def store_upper(queue, first, count, tile, width):
@@ -219,10 +234,10 @@ def tile_concord_graph_gradient_s9_kernel(tc, x, theta_words, theta_scales, v, d
                             in_=upper_out[:, first:first + count, tile * LANES:(tile + width) * LANES])
 
         for t in range(PACK):
-            turn_x(0, t)
+            turn_x(0, t, nc.scalar.copy)
             quantize_x1(0, t)
-            if t == 1:
-                nc.vector.tensor_copy(out=v32[:], in_=v16[:].rearrange("p g t -> p (g t)"))
+            if t == PACK - 2:
+                nc.scalar.copy(out=v32[:], in_=v16[:].rearrange("p g t -> p (g t)"))
         interleave_x2(nc.vector.tensor_copy, 0, HIGH)
         for g in range(GROUPS):
             more = g + 1 < GROUPS
@@ -238,26 +253,20 @@ def tile_concord_graph_gradient_s9_kernel(tc, x, theta_words, theta_scales, v, d
             interleave_r(g, LOW)
             quantize_x2(g, LOW)
             if more:
-                turn_x(g + 1, 0)
-                turn_x(g + 1, 1)
-                quantize_x1(g + 1, 0)
-            quantize_r(g, LOW)
-            if more:
-                quantize_x1(g + 1, 1)
-            residuals(g, HIGH, 0)
-            residuals(g, HIGH, 1)
-            if more:
-                turn_x(g + 1, 2)
-                turn_x(g + 1, 3)
+                for t in range(PACK):
+                    turn_x(g + 1, t, nc.scalar.copy)
             if g == 2:
                 turn_dw()
             if more:
-                quantize_x1(g + 1, 2)
-                quantize_x1(g + 1, 3)
+                quantize_x1(g + 1, 0)
+            quantize_r(g, LOW)
+            if more:
+                for t in range(1, PACK):
+                    quantize_x1(g + 1, t)
             if g == 2:
                 nc.vector.reciprocal(out=neg_inv_w[:], in_=neg_w[:])
-            residuals(g, HIGH, 2)
-            residuals(g, HIGH, 3)
+            for t in range(PACK):
+                residuals(g, HIGH, t)
 
         def upper_transposed(tile):
             bank = take_bank()
@@ -296,18 +305,17 @@ def tile_concord_graph_gradient_s9_kernel(tc, x, theta_words, theta_scales, v, d
                 x2_times_r(bank, g, HIGH, tile, HIGH)
             scale_diag(HIGH, {tile: bank}, tile)
         lower(0, 1)
-        diag_rows(HIGH)
         lower(1, 1)
+        diag_rows(HIGH)
+        upper(0, 0, TILES, nc.scalar.copy)
+        upper(1, 0, TILES, nc.scalar.copy)
+        store_upper(nc.sync, 0, TILES, 0, 2)
         upper_transposed(2)
         lower(2, 1)
         upper_transposed(3)
-        upper(0, 0, TILES)
-        upper(1, 0, TILES)
-        store_upper(nc.sync, 0, TILES, 0, 2)
-        upper(2, 0, TILES)
-        store_upper(nc.sync, 0, TILES, 2, 1)
         lower(3, 2)
-        upper(3, 0, 2)
-        store_upper(nc.sync, 0, 2, 3, 1)
-        upper(3, 2, 2)
-        store_upper(nc.scalar, 2, 2, 3, 1)
+        upper(2, 0, TILES, nc.scalar.copy)
+        upper(3, 0, 2, nc.vector.tensor_copy)
+        store_upper(nc.sync, 0, 2, 2, 2)
+        upper(3, 2, 2, nc.scalar.copy)
+        store_upper(nc.scalar, 2, 2, 2, 2)

@@ -27,7 +27,6 @@ KPASSES = P // PASS
 TILES = HALF // LANES
 BANKS = 8
 LOW, HIGH = 0, 1
-WARM_PASSES = 3
 
 
 def tile_concord_graph_gradient_s9_kernel(tc, x, theta_words, theta_scales, v, d, w, out):
@@ -38,7 +37,7 @@ def tile_concord_graph_gradient_s9_kernel(tc, x, theta_words, theta_scales, v, d
         ctx.enter_context(tc.manual_schedule())
 
         def tiles(name, count, shape, dtype):
-            return [sb.tile(shape, dtype, name="%s%d" % (name, n), align_bytes=64) for n in range(count)]
+            return [sb.tile(shape, dtype, name="%s%d" % (name, n), align_bytes=256) for n in range(count)]
 
         banks = [ps.tile([LANES, HALF], F32, name="bank%d" % n) for n in range(BANKS)]
         taken = []
@@ -47,21 +46,18 @@ def tile_concord_graph_gradient_s9_kernel(tc, x, theta_words, theta_scales, v, d
             taken.append(banks[len(taken) % BANKS])
             return taken[-1]
 
-        ident = sb.tile([LANES, LANES], F32, name="ident", align_bytes=64)
-        ident16 = sb.tile([LANES, LANES], BF16, name="ident16", align_bytes=64)
+        ident = sb.tile([LANES, LANES], F32, name="ident", align_bytes=256)
+        ident16 = sb.tile([LANES, LANES], BF16, name="ident16", align_bytes=256)
         xs = tiles("xs", GROUPS, [LANES, PACK * P], BF16)
         theta = tiles("theta", 2, [LANES, KPASSES, 2 * HALF], U8)
-        theta_plane = sb.tile([LANES, KPASSES, P], U8, name="theta_plane", align_bytes=64)
-        v16 = sb.tile([LANES, GROUPS, PACK], BF16, name="v16", align_bytes=64)
-        v32 = sb.tile([LANES, GROUPS * PACK], F32, name="v32", align_bytes=64)
-        dw_rows = sb.tile([LANES, LANES], BF16, name="dw_rows", align_bytes=64)
-        d_col = sb.tile([LANES, 2 * TILES], F32, name="d_col", align_bytes=64)
-        neg_w = sb.tile([LANES, 2 * TILES], F32, name="neg_w", align_bytes=64)
-        neg_inv_w = sb.tile([LANES, 2 * TILES], F32, name="neg_inv_w", align_bytes=64)
-        d_row = sb.tile([LANES, HALF], BF16, name="d_row", align_bytes=64)
-        warm_in = sb.tile([LANES, PASS], BF16, name="warm_in", align_bytes=64)
-        warm_codes = sb.tile([LANES, HALF + LANES], U32, name="warm_codes", align_bytes=64)
-        warm_plane = sb.tile([LANES, HALF + LANES], U8, name="warm_plane", align_bytes=64)
+        theta_plane = sb.tile([LANES, KPASSES, P], U8, name="theta_plane", align_bytes=256)
+        v16 = sb.tile([LANES, GROUPS, PACK], BF16, name="v16", align_bytes=256)
+        v32 = sb.tile([LANES, GROUPS * PACK], F32, name="v32", align_bytes=256)
+        dw_rows = sb.tile([LANES, LANES], BF16, name="dw_rows", align_bytes=256)
+        d_col = sb.tile([LANES, 2 * TILES], F32, name="d_col", align_bytes=256)
+        neg_w = sb.tile([LANES, 2 * TILES], F32, name="neg_w", align_bytes=256)
+        neg_inv_w = sb.tile([LANES, 2 * TILES], F32, name="neg_inv_w", align_bytes=256)
+        d_row = sb.tile([LANES, HALF], BF16, name="d_row", align_bytes=256)
         x1_in = tiles("x1_in", PACK, [LANES, KPASSES * PASS], BF16)
         x1_codes = tiles("x1_codes", 2 * PACK, [LANES, KPASSES * LANES], U32)
         x1_plane = tiles("x1_plane", 2 * PACK, [LANES, KPASSES * LANES], U8)
@@ -76,7 +72,7 @@ def tile_concord_graph_gradient_s9_kernel(tc, x, theta_words, theta_scales, v, d
         upper_t = tiles("upper_t", TILES, [LANES, HALF], F32)
         diag_out = tiles("diag_out", 2 * TILES, [LANES, HALF], F32)
         lower_out = tiles("lower_out", TILES, [LANES, HALF], F32)
-        upper_out = sb.tile([LANES, TILES, HALF], F32, name="upper_out", align_bytes=64)
+        upper_out = sb.tile([LANES, TILES, HALF], F32, name="upper_out", align_bytes=256)
 
         def load_x(g, t0, t1):
             rows = x[g * PASS:(g + 1) * PASS, :].rearrange("(p t) k -> p (t k)", t=PACK)
@@ -87,9 +83,7 @@ def tile_concord_graph_gradient_s9_kernel(tc, x, theta_words, theta_scales, v, d
             nc.sync.dma_start(out=theta[half][:].bitcast(I32), in_=words.bitcast(I32))
 
         nc.gpsimd.memset(theta_plane[:].rearrange("p h n -> p (h n)").bitcast(I32), 0)
-        nc.gpsimd.memset(warm_in[:], 0.0)
         make_identity(nc, ident[:])
-        nc.gpsimd.dma_start(out=v16[:], in_=v.rearrange("(g p t) -> p g t", g=GROUPS, t=PACK))
         nc.gpsimd.memset(dw_rows[:], 0.0)
         load_x(0, 0, 1)
         load_x(0, 1, 2)
@@ -99,6 +93,7 @@ def tile_concord_graph_gradient_s9_kernel(tc, x, theta_words, theta_scales, v, d
         load_x(0, 2, 3)
         load_x(0, 3, 4)
         load_theta(LOW)
+        nc.sync.dma_start(out=v16[:], in_=v.rearrange("(g p t) -> p g t", g=GROUPS, t=PACK))
         load_x(1, 0, 2)
         load_x(1, 2, 4)
         load_theta(HIGH)
@@ -107,16 +102,9 @@ def tile_concord_graph_gradient_s9_kernel(tc, x, theta_words, theta_scales, v, d
         nc.sync.dma_start(out=dw_rows[0:8, :], in_=d.rearrange("(c j) -> c j", j=LANES))
         nc.sync.dma_start(out=dw_rows[8:16, :], in_=w.rearrange("(c j) -> c j", j=LANES))
         nc.sync.dma_start(out=d_row[:], in_=d[0:HALF].partition_broadcast(LANES))
+        nc.gpsimd.tensor_copy(out=v32[:], in_=v16[:].rearrange("p g t -> p (g t)"))
         nc.scalar.activation(out=ident16[:], in_=ident[:], func=COPY)
 
-        nc.vector.quantize_mx(out=warm_codes[:, HALF:].bitcast(E4M3), scales=warm_plane[:, HALF:], in_=warm_in[:])
-        for n in range(TILES):
-            cols = slice(n * LANES, (n + 1) * LANES)
-            nc.vector.quantize_mx(out=warm_codes[:, cols].bitcast(E5M2), scales=warm_plane[:, cols], in_=warm_in[:])
-        for n in range(WARM_PASSES):
-            nc.tensor.matmul_mx(out=banks[-1][:], lhsT=warm_codes[:, HALF:].bitcast(E4M3), lhsT_scale=warm_plane[:, HALF:],
-                                rhs=warm_codes[:, 0:HALF].bitcast(E5M2), rhs_scale=warm_plane[:, 0:HALF],
-                                start=True, stop=True)
 
         def turn_x(g, t, engine_copy):
             bank = take_bank()
@@ -236,8 +224,6 @@ def tile_concord_graph_gradient_s9_kernel(tc, x, theta_words, theta_scales, v, d
         for t in range(PACK):
             turn_x(0, t, nc.scalar.copy)
             quantize_x1(0, t)
-            if t == PACK - 2:
-                nc.scalar.copy(out=v32[:], in_=v16[:].rearrange("p g t -> p (g t)"))
         interleave_x2(nc.vector.tensor_copy, 0, HIGH)
         for g in range(GROUPS):
             more = g + 1 < GROUPS
@@ -258,11 +244,9 @@ def tile_concord_graph_gradient_s9_kernel(tc, x, theta_words, theta_scales, v, d
             if g == 2:
                 turn_dw()
             if more:
-                quantize_x1(g + 1, 0)
-            quantize_r(g, LOW)
-            if more:
-                for t in range(1, PACK):
+                for t in range(PACK):
                     quantize_x1(g + 1, t)
+            quantize_r(g, LOW)
             if g == 2:
                 nc.vector.reciprocal(out=neg_inv_w[:], in_=neg_w[:])
             for t in range(PACK):
@@ -295,15 +279,21 @@ def tile_concord_graph_gradient_s9_kernel(tc, x, theta_words, theta_scales, v, d
         for tile in range(TILES):
             scale_diag(LOW, low_banks, tile)
         interleave_x2(nc.vector.tensor_copy, 3, HIGH)
-        upper_transposed(0)
+        pair = [take_bank(), take_bank()]
+        for g in range(GROUPS):
+            for tile in range(2):
+                r_times_x2(pair[tile], g, tile)
+        nc.vector.tensor_tensor(out=upper_t[0][:], in0=pair[0][:], in1=d_row[:], op=MULT)
         quantize_x2(3, HIGH)
-        upper_transposed(1)
+        nc.vector.tensor_tensor(out=upper_t[1][:], in0=pair[1][:], in1=d_row[:], op=MULT)
         diag_rows(LOW)
-        for tile in range(TILES):
-            bank = take_bank()
+        for first in range(0, TILES, 2):
+            pair = {first: take_bank(), first + 1: take_bank()}
             for g in range(GROUPS):
-                x2_times_r(bank, g, HIGH, tile, HIGH)
-            scale_diag(HIGH, {tile: bank}, tile)
+                for tile in pair:
+                    x2_times_r(pair[tile], g, HIGH, tile, HIGH)
+            for tile in pair:
+                scale_diag(HIGH, pair, tile)
         lower(0, 1)
         lower(1, 1)
         diag_rows(HIGH)

from contextlib import ExitStack

import concourse.mybir as mybir
from concourse.masks import make_identity

M, P = 2048, 1024
FLOPS = 2 * M * P * P * 2

F32 = mybir.dt.float32
BF16 = mybir.dt.bfloat16
I32 = mybir.dt.int32
U32 = mybir.dt.uint32
U8 = mybir.dt.uint8
E4M3 = mybir.dt.float8_e4m3fn_x4
E5M2 = mybir.dt.float8_e5m2_x4
E2M1 = mybir.dt.float4_e2m1fn_x4
COPY = mybir.ActivationFunctionType.Copy
MULT = mybir.AluOpType.mult
ADD = mybir.AluOpType.add

LANES = 128
PACK = 4
PASS = LANES * PACK
HALF = P // 2
GROUPS = M // PASS
KPASSES = P // PASS
TILES = HALF // LANES
BANKS = 8
LOW, HIGH = 0, 1


def tile_concord_graph_gradient_s9_kernel(tc, x, theta_words, theta_scales, v, d, w, out):
    nc = tc.nc
    with ExitStack() as ctx:
        sb = ctx.enter_context(tc.tile_pool(name="sb", bufs=1))
        ps = ctx.enter_context(tc.psum_pool(name="ps", bufs=1))
        ctx.enter_context(tc.manual_schedule())

        def tiles(name, count, shape, dtype):
            return [sb.tile(shape, dtype, name="%s%d" % (name, n), align_bytes=256) for n in range(count)]

        banks = [ps.tile([LANES, HALF], F32, name="bank%d" % n) for n in range(BANKS)]
        taken = []

        def take_bank():
            taken.append(banks[len(taken) % BANKS])
            return taken[-1]

        ident = sb.tile([LANES, LANES], F32, name="ident", align_bytes=256)
        ident16 = sb.tile([LANES, LANES], BF16, name="ident16", align_bytes=256)
        xs = tiles("xs", GROUPS, [LANES, PACK * P], BF16)
        theta = tiles("theta", 2, [LANES, KPASSES, 2 * HALF], U8)
        theta_plane = sb.tile([LANES, KPASSES, P], U8, name="theta_plane", align_bytes=256)
        v16 = sb.tile([LANES, GROUPS, PACK], BF16, name="v16", align_bytes=256)
        v32 = sb.tile([LANES, GROUPS * PACK], F32, name="v32", align_bytes=256)
        dw_rows = sb.tile([LANES, LANES], BF16, name="dw_rows", align_bytes=256)
        d_col = sb.tile([LANES, 2 * TILES], F32, name="d_col", align_bytes=256)
        neg_w = sb.tile([LANES, 2 * TILES], F32, name="neg_w", align_bytes=256)
        neg_inv_w = sb.tile([LANES, 2 * TILES], F32, name="neg_inv_w", align_bytes=256)
        d_row = sb.tile([LANES, HALF], BF16, name="d_row", align_bytes=256)
        x1_in = tiles("x1_in", PACK, [LANES, KPASSES * PASS], BF16)
        x1_codes = tiles("x1_codes", 2 * PACK, [LANES, KPASSES * LANES], U32)
        x1_plane = tiles("x1_plane", 2 * PACK, [LANES, KPASSES * LANES], U8)
        r_rows = tiles("r_rows", 3, [LANES, PACK * HALF], BF16)
        r_in = tiles("r_in", 2, [LANES, PACK * HALF], BF16)
        x2_in = tiles("x2_in", 3, [LANES, PACK * HALF], BF16)
        r_codes = tiles("r_codes", 2 * GROUPS, [LANES, HALF], U32)
        r_plane = tiles("r_plane", 2 * GROUPS, [LANES, HALF], U8)
        x2_codes = tiles("x2_codes", 2 * GROUPS, [LANES, HALF], U32)
        x2_plane = tiles("x2_plane", 2 * GROUPS, [LANES, HALF], U8)
        scaled = tiles("scaled", 2 * TILES, [LANES, HALF], F32)
        upper_t = tiles("upper_t", TILES, [LANES, HALF], F32)
        diag_out = tiles("diag_out", 2 * TILES, [LANES, HALF], F32)
        lower_out = tiles("lower_out", TILES, [LANES, HALF], F32)
        upper_out = sb.tile([LANES, TILES, HALF], F32, name="upper_out", align_bytes=256)

        def load_x(g, t0, t1):
            rows = x[g * PASS:(g + 1) * PASS, :].rearrange("(p t) k -> p (t k)", t=PACK)
            nc.sync.dma_start(out=xs[g][:, t0 * P:t1 * P], in_=rows[:, t0 * P:t1 * P])

        def load_theta(half):
            words = theta_words.rearrange("h p b -> p h b")[:, :, half * 2 * HALF:(half + 1) * 2 * HALF]
            nc.sync.dma_start(out=theta[half][:].bitcast(I32), in_=words.bitcast(I32))

        nc.gpsimd.memset(theta_plane[:].rearrange("p h n -> p (h n)").bitcast(I32), 0)
        make_identity(nc, ident[:])
        nc.gpsimd.memset(dw_rows[:], 0.0)
        load_x(0, 0, 1)
        load_x(0, 1, 2)
        for q in range(4):
            rows = theta_scales[:, 4 * q:4 * q + 4, :].rearrange("h r n -> r h n")
            nc.sync.dma_start(out=theta_plane[32 * q:32 * q + 4, :, :].bitcast(I32), in_=rows.bitcast(I32))
        load_x(0, 2, 3)
        load_x(0, 3, 4)
        load_theta(LOW)
        nc.sync.dma_start(out=v16[:], in_=v.rearrange("(g p t) -> p g t", g=GROUPS, t=PACK))
        load_x(1, 0, 2)
        load_x(1, 2, 4)
        load_theta(HIGH)
        load_x(2, 0, 4)
        load_x(3, 0, 4)
        nc.sync.dma_start(out=dw_rows[0:8, :], in_=d.rearrange("(c j) -> c j", j=LANES))
        nc.sync.dma_start(out=dw_rows[8:16, :], in_=w.rearrange("(c j) -> c j", j=LANES))
        nc.sync.dma_start(out=d_row[:], in_=d[0:HALF].partition_broadcast(LANES))
        nc.gpsimd.tensor_copy(out=v32[:], in_=v16[:].rearrange("p g t -> p (g t)"))
        nc.scalar.activation(out=ident16[:], in_=ident[:], func=COPY)


        def turn_x(g, t, engine_copy):
            bank = take_bank()
            words = xs[g][:].bitcast(F32)
            for h in range(KPASSES):
                for u in range(2):
                    first = t * (P // 2) + h * 2 * LANES
                    n = 2 * h + u
                    nc.tensor.transpose(bank[:, n * LANES:(n + 1) * LANES],
                                        words[:, first + u:first + 2 * LANES:2], ident[:])
            engine_copy(out=x1_in[t][:].bitcast(F32).rearrange("p (h r u) -> p h r u", h=KPASSES, u=2),
                           in_=bank[:].rearrange("p (h u r) -> p h r u", h=KPASSES, u=2))

        def quantize_x1(g, t):
            n = (g * PACK + t) % (2 * PACK)
            nc.vector.quantize_mx(out=x1_codes[n][:].bitcast(E4M3), scales=x1_plane[n][:], in_=x1_in[t][:])

        def residuals(g, half, t):
            bank = take_bank()
            n = (g * PACK + t) % (2 * PACK)
            for h in range(KPASSES):
                cols = slice(h * LANES, (h + 1) * LANES)
                nc.tensor.matmul_mx(out=bank[:], lhsT=x1_codes[n][:, cols].bitcast(E4M3), lhsT_scale=x1_plane[n][:, cols],
                                    rhs=theta[half][:, h, :].bitcast(E2M1),
                                    rhs_scale=theta_plane[:, h, half * HALF:(half + 1) * HALF],
                                    start=(h == 0), stop=(h == KPASSES - 1))
            rows = r_rows[(2 * g + half) % 3]
            nc.scalar.activation(out=rows[:, t * HALF:(t + 1) * HALF], in_=bank[:], func=COPY,
                                 scale=v32[:, g * PACK + t:g * PACK + t + 1])

        def interleave(engine_copy, dst, src_rows):
            engine_copy(out=dst[:].rearrange("p (c i t) -> p c t i", i=4, t=PACK),
                        in_=src_rows.rearrange("p t (c i) -> p c t i", i=4))

        def interleave_r(g, half):
            rows = r_rows[(2 * g + half) % 3][:].rearrange("p (t n) -> p t n", t=PACK)
            interleave(nc.vector.tensor_copy, r_in[half], rows)

        def quantize_r(g, half):
            n = 2 * g + half
            nc.vector.quantize_mx(out=r_codes[n][:].bitcast(E5M2), scales=r_plane[n][:], in_=r_in[half][:])

        def interleave_x2(engine_copy, g, half):
            rows = xs[g][:].rearrange("p (t k) -> p t k", t=PACK)[:, :, half * HALF:(half + 1) * HALF]
            interleave(engine_copy, x2_in[(half + g) % 3], rows)

        def quantize_x2(g, half):
            n = 2 * g + half
            nc.vector.quantize_mx(out=x2_codes[n][:].bitcast(E4M3), scales=x2_plane[n][:],
                                  in_=x2_in[(half + g) % 3][:])

        def x2_times_r(bank, g, x2_half, tile, r_half):
            cols = slice(tile * LANES, (tile + 1) * LANES)
            a, b = 2 * g + x2_half, 2 * g + r_half
            nc.tensor.matmul_mx(out=bank[:], lhsT=x2_codes[a][:, cols].bitcast(E4M3), lhsT_scale=x2_plane[a][:, cols],
                                rhs=r_codes[b][:].bitcast(E5M2), rhs_scale=r_plane[b][:],
                                start=(g == 0), stop=(g == GROUPS - 1))

        def r_times_x2(bank, g, tile):
            cols = slice(tile * LANES, (tile + 1) * LANES)
            a, b = 2 * g + HIGH, 2 * g + LOW
            nc.tensor.matmul_mx(out=bank[:], lhsT=r_codes[a][:, cols].bitcast(E5M2), lhsT_scale=r_plane[a][:, cols],
                                rhs=x2_codes[b][:].bitcast(E4M3), rhs_scale=x2_plane[b][:],
                                start=(g == 0), stop=(g == GROUPS - 1))

        def turn_dw():
            bank = take_bank()
            cols = bank[:].bitcast(BF16)[:, 0:LANES]
            nc.tensor.transpose(cols, dw_rows[:], ident16[:])
            nc.scalar.copy(out=d_col[:], in_=cols[:, 0:8])
            nc.scalar.activation(out=neg_w[:], in_=cols[:, 8:16], func=COPY, scale=-1.0)

        def scale_diag(half, group_banks, tile):
            n = half * TILES + tile
            nc.scalar.activation(out=scaled[n][:], in_=group_banks[tile][:], func=COPY, scale=d_col[:, n:n + 1])

        def turn_diag(half, tile):
            bank = take_bank()
            for j in range(TILES):
                nc.tensor.transpose(bank[:, j * LANES:(j + 1) * LANES],
                                    scaled[half * TILES + j][:, tile * LANES:(tile + 1) * LANES], ident[:])
            n = half * TILES + tile
            nc.vector.tensor_tensor(out=diag_out[n][:], in0=bank[:], in1=scaled[n][:], op=ADD)

        def finish_diag(half, tile):
            n = half * TILES + tile
            block = diag_out[n][:, tile * LANES:(tile + 1) * LANES]
            nc.vector.scalar_tensor_tensor(out=block, in0=ident[:], scalar=neg_inv_w[:, n:n + 1], in1=block,
                                           op0=MULT, op1=ADD)
            nc.sync.dma_start(out=out[n * LANES:(n + 1) * LANES, half * HALF:(half + 1) * HALF], in_=diag_out[n][:])

        def lower(tile, parts):
            bank = take_bank()
            for g in range(GROUPS):
                x2_times_r(bank, g, HIGH, tile, LOW)
            n = TILES + tile
            width = HALF // parts
            for part in range(parts):
                cols = slice(part * width, (part + 1) * width)
                nc.vector.scalar_tensor_tensor(out=lower_out[tile][:, cols], in0=bank[:, cols], scalar=d_col[:, n:n + 1],
                                               in1=upper_t[tile][:, cols], op0=MULT, op1=ADD)
            nc.sync.dma_start(out=out[n * LANES:(n + 1) * LANES, 0:HALF], in_=lower_out[tile][:])

        def upper(tile, first, count, engine_copy):
            bank = take_bank()
            for i in range(count):
                nc.tensor.transpose(bank[:, i * LANES:(i + 1) * LANES],
                                    lower_out[tile][:, (first + i) * LANES:(first + i + 1) * LANES], ident[:])
            engine_copy(out=upper_out[:, first:first + count, tile * LANES:(tile + 1) * LANES],
                           in_=bank[:, 0:count * LANES].rearrange("p (i c) -> p i c", i=count))

        def store_upper(queue, first, count, tile, width):
            rows = out[first * LANES:(first + count) * LANES, HALF + tile * LANES:HALF + (tile + width) * LANES]
            queue.dma_start(out=rows.rearrange("(i p) c -> p i c", p=LANES),
                            in_=upper_out[:, first:first + count, tile * LANES:(tile + width) * LANES])

        for t in range(PACK):
            turn_x(0, t, nc.scalar.copy)
            quantize_x1(0, t)
        interleave_x2(nc.vector.tensor_copy, 0, HIGH)
        for g in range(GROUPS):
            more = g + 1 < GROUPS
            for t in range(PACK):
                residuals(g, LOW, t)
            if g > 0:
                interleave_r(g - 1, HIGH)
            interleave_x2(nc.vector.tensor_copy, g, LOW)
            if g > 0:
                quantize_r(g - 1, HIGH)
            else:
                quantize_x2(0, HIGH)
            interleave_r(g, LOW)
            quantize_x2(g, LOW)
            if more:
                for t in range(PACK):
                    turn_x(g + 1, t, nc.scalar.copy)
            if g == 2:
                turn_dw()
            if more:
                for t in range(PACK):
                    quantize_x1(g + 1, t)
            quantize_r(g, LOW)
            if g == 2:
                nc.vector.reciprocal(out=neg_inv_w[:], in_=neg_w[:])
            for t in range(PACK):
                residuals(g, HIGH, t)

        def upper_transposed(tile):
            bank = take_bank()
            for g in range(GROUPS):
                r_times_x2(bank, g, tile)
            nc.vector.tensor_tensor(out=upper_t[tile][:], in0=bank[:], in1=d_row[:], op=MULT)

        def diag_rows(half):
            for tile in range(TILES):
                turn_diag(half, tile)
                if tile > 0:
                    finish_diag(half, tile - 1)
            finish_diag(half, TILES - 1)

        last = GROUPS - 1
        interleave_r(last, HIGH)
        interleave_x2(nc.scalar.copy, 1, HIGH)
        interleave_x2(nc.vector.tensor_copy, 2, HIGH)
        quantize_r(last, HIGH)
        low_banks = [take_bank() for tile in range(TILES)]
        for g in range(GROUPS):
            for tile in range(TILES):
                x2_times_r(low_banks[tile], g, LOW, tile, LOW)
        quantize_x2(2, HIGH)
        quantize_x2(1, HIGH)
        for tile in range(TILES):
            scale_diag(LOW, low_banks, tile)
        interleave_x2(nc.vector.tensor_copy, 3, HIGH)
        pair = [take_bank(), take_bank()]
        for g in range(GROUPS):
            for tile in range(2):
                r_times_x2(pair[tile], g, tile)
        nc.vector.tensor_tensor(out=upper_t[0][:], in0=pair[0][:], in1=d_row[:], op=MULT)
        quantize_x2(3, HIGH)
        nc.vector.tensor_tensor(out=upper_t[1][:], in0=pair[1][:], in1=d_row[:], op=MULT)
        diag_rows(LOW)
        for first in range(0, TILES, 2):
            pair = {first: take_bank(), first + 1: take_bank()}
            for g in range(GROUPS):
                for tile in pair:
                    x2_times_r(pair[tile], g, HIGH, tile, HIGH)
            for tile in pair:
                scale_diag(HIGH, pair, tile)
        lower(0, 1)
        lower(1, 1)
        diag_rows(HIGH)
        upper(0, 0, TILES, nc.scalar.copy)
        upper(1, 0, TILES, nc.scalar.copy)
        store_upper(nc.sync, 0, TILES, 0, 2)
        upper_transposed(2)
        lower(2, 1)
        upper_transposed(3)
        lower(3, 2)
        upper(2, 0, TILES, nc.scalar.copy)
        upper(3, 0, 2, nc.vector.tensor_copy)
        store_upper(nc.sync, 0, 2, 2, 2)
        upper(3, 2, 2, nc.scalar.copy)
        store_upper(nc.scalar, 2, 2, 2, 2)
